import numpy as np
import ml_dtypes


def mxq(x, axis, fmt="e4m3"):
    dtype, down = {"e4m3": (ml_dtypes.float8_e4m3fn, 7), "e5m2": (ml_dtypes.float8_e5m2, 14)}[fmt]
    v = np.moveaxis(np.asarray(x, np.float32).astype(ml_dtypes.bfloat16).astype(np.float64), axis, -1)
    blocks = v.reshape(v.shape[:-1] + (-1, 32))
    amax = np.abs(blocks).max(-1, keepdims=True)
    byte = np.maximum(np.where(amax > 0, np.frexp(amax)[1] - 1 + 127, 0) - down, 1)
    scale = np.exp2(byte - 127.0)
    codes = (blocks / scale).astype(np.float32).astype(dtype).astype(np.float64)
    return np.moveaxis((codes * scale).reshape(v.shape), -1, axis)


WIDE = False


def mx_kscale(k):
    if not WIDE:
        return np.ones(k)
    levels = np.array([10, -10, 5, -5, 0])
    if k % 512:
        return np.exp2(np.random.permutation(np.resize(levels, k // 32))).repeat(32)
    a = np.empty((k // 512, 16))
    for p in range(k // 512):
        a[p, :8] = np.random.permutation(np.resize(levels, 8))
        for g in range(8):
            far = levels[np.abs(levels - a[p, g]) >= 10]
            a[p, g + 8] = far[np.random.randint(len(far))]
    return np.exp2(a.ravel()).repeat(32)


def f64(x):
    return np.asarray(x).astype(np.float64)


def striped(idx):
    return np.tile(np.asarray(idx).reshape(-1, 16).T, (8, 1)).astype(np.uint16)


def unstriped(offs):
    return offs[:16].T.reshape(-1).astype(np.int64)


E2M1 = np.array([0.0, 0.5, 1.0, 1.5, 2.0, 3.0, 4.0, 6.0, -0.0, -0.5, -1.0, -1.5, -2.0, -3.0, -4.0, -6.0])


def pack_weight(w, fmt):
    k, n = w.shape
    w = f64(np.asarray(w, np.float32).astype(ml_dtypes.bfloat16)).reshape(k // 32, 32, n)
    amax = np.abs(w).max(1)
    if fmt == "e4m3":
        byte = np.frexp(amax)[1] - 1 + 127 - 7
    else:
        mant, ex = np.frexp(amax / 6.0)
        byte = np.where(mant > 0.5, ex, ex - 1) + 127
    byte = np.clip(np.where(amax > 0, byte, 1), 1, 254)
    scaled = (w * np.exp2(127.0 - byte)[:, None, :]).reshape(k, n).astype(np.float32)
    by_word = np.ascontiguousarray(scaled.reshape(k // 512, 128, 4, n).transpose(0, 1, 3, 2))
    if fmt == "e4m3":
        words = by_word.astype(ml_dtypes.float8_e4m3fn).view(np.uint8)
    else:
        c = by_word.astype(ml_dtypes.float4_e2m1fn).view(np.uint8) & 0xF
        words = (c[..., 0::2] | (c[..., 1::2] << 4)).reshape(k // 512, 128, 2 * n)
    return np.ascontiguousarray(words), np.ascontiguousarray(byte.astype(np.uint8).reshape(k // 512, 16, n))


def unpack_weight(words, scales, fmt):
    g, _, n = scales.shape
    words = np.ascontiguousarray(words).reshape(g, 128, n, -1)
    if fmt == "e4m3":
        vals = words.view(ml_dtypes.float8_e4m3fn).astype(np.float64)
    else:
        nib = np.empty((g, 128, n, 4), np.uint8)
        nib[..., 0::2] = words & 0xF
        nib[..., 1::2] = words >> 4
        vals = E2M1[nib]
    vals = vals * np.repeat(np.exp2(scales.astype(np.float64) - 127.0), 8, axis=1)[..., None]
    return vals.transpose(0, 1, 3, 2).reshape(g * 512, n)


def softplus(v):
    return np.log(1.0 + np.exp(v))


D, E, T, I, Q, G = 512, 512, 2048, 512, 128, 64


def setup_inputs():
    n = np.random.standard_normal
    idx = np.random.permutation(T)[:I]
    fd = mx_kscale(D)
    fi = mx_kscale(I)
    ti = np.ones(T)
    ti[idx] = fi
    keysp = pack_weight(n((D, T)) / fd[:, None], "e2m1")
    return {
        "query": (n((D, Q)) * 0.8 / np.sqrt(D) * fd[:, None]).astype(np.float32),
        "query2": (n((D, Q)) * 1.0 / np.sqrt(D) * fd[:, None]).astype(np.float32),
        "keys_words": keysp[0],
        "keys_scales": keysp[1],
        "reserve": (np.random.uniform(2.0, 10.0, (Q, 1))).astype(np.float32),
        "os": (np.random.uniform(4.0, 16.0, (1, I)) * fi).astype(np.float32),
        "vals": (n((E, T)) / ti).astype(np.float32),
        "offs": striped(idx),
    }


def reference(query, query2, keys_words, keys_scales, reserve, os, vals, offs):
    idx = unstriped(offs)
    keysu = unpack_weight(keys_words, keys_scales, "e2m1")
    queryq = mxq(f64(query), 0, "e4m3")
    keysidxg = keysu[:, idx]
    a = queryq.T @ keysidxg
    query2q = mxq(f64(query2), 0, "e4m3")
    b = query2q.T @ keysidxg
    m1 = b.reshape(Q, G, I // G).mean(axis=2)
    q0 = softplus(m1 * 3.0)
    z = np.sum(q0, axis=1, keepdims=True) + f64(reserve)
    pa = np.exp(a)
    s = pa.reshape(Q, G, I // G).sum(axis=2)
    r = q0 / s / z
    rr = np.repeat(r, I // G, axis=1)
    w = pa * rr
    wo1 = w * f64(os)
    wt1 = wo1.T
    vt1 = f64(vals)[:, idx].T
    wt1q = mxq(wt1, 0, "e4m3")
    vt1q = mxq(vt1, 0, "e4m3")
    o = wt1q.T @ vt1q
    return o

@@ -1,0 +1,205 @@
+from contextlib import ExitStack
+
+import concourse.mybir as mybir
+from concourse.masks import make_identity
+
+D, E, T, I, Q, G = 512, 512, 2048, 512, 128, 64
+FLOPS = 2 * Q * I * D * 2 + 2 * Q * I * E
+
+F32 = mybir.dt.float32
+BF16 = mybir.dt.bfloat16
+I32 = mybir.dt.int32
+U32 = mybir.dt.uint32
+U16 = mybir.dt.uint16
+U8 = mybir.dt.uint8
+FP8X4 = mybir.dt.float8_e4m3fn_x4
+FP4X4 = mybir.dt.float4_e2m1fn_x4
+ACT = mybir.ActivationFunctionType
+ALU = mybir.AluOpType
+AXIS = mybir.AxisListType
+
+P = 128
+PACK = 4
+PAGE = I // G
+HALVES = PAGE // PACK
+BLOCKS = E // P
+
+
+def tile_attend_pagequotas_kernel(tc, query, query2, keys_words, keys_scales, reserve, slot_factors, vals, offs, out):
+    nc = tc.nc
+    with ExitStack() as ctx:
+        held = ctx.enter_context(tc.tile_pool(name="held", bufs=1))
+        psum = ctx.enter_context(tc.psum_pool(name="psum", bufs=1))
+        turn = ctx.enter_context(tc.psum_pool(name="turn", bufs=2))
+
+        offsets = held.tile([P, I // 16], U16, name="offsets")
+        nc.sync.dma_start(offsets[:], offs)
+
+        key_bytes = held.tile([P, T], U8, name="key_bytes")
+        nc.gpsimd.memset(key_bytes[:].bitcast(I32), 0)
+        identity = held.tile([P, P], F32, name="identity")
+        make_identity(nc, identity[:])
+        key_words = held.tile([P, T], U16, name="key_words", tag="slot1")
+        nc.sync.dma_start(key_words[:].bitcast(I32), keys_words[0].bitcast(I32))
+        for r in range(4):
+            nc.scalar.dma_start(key_bytes[r:P:32, :].bitcast(I32), keys_scales[0, r:16:4, :].bitcast(I32))
+
+        q_raw = []
+        for n, source in enumerate((query, query2)):
+            raw = held.tile([P, PACK, Q], F32, name="q_raw%d" % n, tag="slot%d" % (n + 2))
+            nc.sync.dma_start(raw[:], source.rearrange("(p j) q -> p j q", j=PACK))
+            q_raw.append(raw)
+
+        factor_cols = held.tile([P, PACK], F32, name="factor_cols")
+        nc.gpsimd.dma_start(factor_cols[:], slot_factors.rearrange("o (p t) -> (o p) t", t=PACK))
+        row_reserve = held.tile([P, 1], F32, name="row_reserve")
+        nc.gpsimd.dma_start(row_reserve[:], reserve)
+
+        pools = []
+
+        def load_values(c):
+            pool_c = held.tile([P, T], F32, name="vals%d" % c, tag="slot%d" % c)
+            nc.sync.dma_start(pool_c[:], vals[c * P : (c + 1) * P, :])
+            pools.append(pool_c)
+
+        load_values(0)
+
+        listed_words = held.tile([P, I], U16, name="listed_words", align_bytes=64)
+        nc.vector.tensor_copy(listed_words[:], key_words[:].indirect(offsets[:]))
+        listed_bytes = held.tile([P, I], U8, name="listed_bytes", align_bytes=64)
+        nc.vector.tensor_copy(listed_bytes[:], key_bytes[:].indirect(offsets[:]))
+
+        scores = []
+        for n in range(2):
+            grouped = held.tile([P, Q, PACK], BF16, name="q_grouped%d" % n, align_bytes=64)
+            nc.scalar.activation(grouped[:], q_raw[n][:].rearrange("p j q -> p q j"), ACT.Copy)
+            codes = held.tile([P, Q], U32, name="q_codes%d" % n, align_bytes=64)
+            scales = held.tile([P, Q], U8, name="q_scales%d" % n, align_bytes=64)
+            nc.vector.quantize_mx(
+                out=codes[:].bitcast(FP8X4), scales=scales[:], in_=grouped[:].rearrange("p q j -> p (q j)")
+            )
+            bank = psum.tile([P, I], F32, name="scores%d" % n)
+            nc.tensor.matmul_mx(
+                out=bank[:],
+                lhsT=codes[:].bitcast(FP8X4),
+                lhsT_scale=scales[:],
+                rhs=listed_words[:].bitcast(FP4X4),
+                rhs_scale=listed_bytes[:],
+                start=True,
+                stop=True,
+            )
+            scores.append(bank)
+        a, b = scores
+        for c in range(1, BLOCKS):
+            load_values(c)
+
+        v_codes = held.tile([P, E], U32, name="v_codes", align_bytes=64)
+        v_scales = held.tile([P, E], U8, name="v_scales", align_bytes=64)
+
+        def values_block(c):
+            listed = held.tile([P, I], BF16, name="v_listed%d" % c, align_bytes=64)
+            nc.vector.tensor_copy(listed[:], pools[c][:].indirect(offsets[:]))
+            pairs = listed[:].bitcast(F32)
+            turned = turn.tile([P, 2, P], F32, name="v_turned")
+            for u in range(2):
+                nc.tensor.transpose(turned[:, u, :], pairs[:, u : I // 2 : 2], identity[:])
+            grouped = held.tile([P, P * PACK], BF16, name="v_grouped%d" % c, align_bytes=64)
+            nc.scalar.copy(
+                grouped[:].bitcast(F32).rearrange("p (e u) -> p e u", u=2), turned[:].rearrange("p u e -> p e u")
+            )
+            cols = slice(c * P, (c + 1) * P)
+            nc.vector.quantize_mx(out=v_codes[:, cols].bitcast(FP8X4), scales=v_scales[:, cols], in_=grouped[:])
+
+        page_max = held.tile([P, G], F32, name="page_max")
+        nc.vector.tensor_reduce(page_max[:], a[:].rearrange("q (g j) -> q g j", j=PAGE), AXIS.X, ALU.max)
+        shifted = held.tile([P, PACK, G, HALVES], F32, name="shifted")
+        nc.vector.tensor_tensor(
+            shifted[:],
+            a[:].rearrange("q (g h t) -> q t g h", h=HALVES, t=PACK),
+            page_max[:].unsqueeze(1).unsqueeze(3).to_broadcast([P, PACK, G, HALVES]),
+            ALU.subtract,
+        )
+        b_sum = held.tile([P, G], F32, name="b_sum")
+        nc.vector.tensor_reduce(b_sum[:], b[:].rearrange("q (g j) -> q g j", j=PAGE), AXIS.X, ALU.add)
+
+        values_block(0)
+
+        size = held.tile([P, G], F32, name="size")
+        nc.scalar.activation(size[:], b_sum[:], ACT.Abs, scale=3.0 / PAGE)
+        tail = held.tile([P, G], F32, name="tail")
+        nc.scalar.activation(tail[:], size[:], ACT.Exp, scale=-1.0)
+        pa = held.tile([P, PACK, G, HALVES], F32, name="pa")
+        nc.scalar.activation(pa[:], shifted[:], ACT.Exp)
+        positive = held.tile([P, G + 1], F32, name="positive")
+        nc.scalar.activation(positive[:, 0:G], b_sum[:], ACT.Relu, scale=3.0 / PAGE)
+        nc.scalar.copy(positive[:, G : G + 1], row_reserve[:])
+        log_part = held.tile([P, G + 1], F32, name="log_part")
+        nc.vector.memset(log_part[:, G : G + 1], 0.0)
+        nc.scalar.activation(log_part[:, 0:G], tail[:], ACT.Ln, bias=1.0)
+
+        page_sum = held.tile([P, G], F32, name="page_sum")
+        nc.vector.tensor_reduce(page_sum[:], pa[:].rearrange("q t g h -> q g t h"), AXIS.XY, ALU.add)
+        inv_page_sum = held.tile([P, G], F32, name="inv_page_sum")
+        nc.vector.reciprocal(inv_page_sum[:], page_sum[:])
+
+        pa_turned = psum.tile([P, PACK, Q], F32, name="pa_turned")
+        for t in range(PACK):
+            nc.tensor.transpose(pa_turned[:, t, :], pa[:, t, :, :].rearrange("q g h -> q (g h)"), identity[:])
+        pa_os = held.tile([P, PACK, Q], F32, name="pa_os")
+        for t in range(PACK):
+            nc.scalar.activation(pa_os[:, t, :], pa_turned[:, t, :], ACT.Copy, scale=factor_cols[:, t : t + 1])
+
+        values_block(1)
+
+        quota = held.tile([P, G + 1], F32, name="quota")
+        z = held.tile([P, 1], F32, name="z")
+        nc.vector.scalar_tensor_tensor(quota[:], log_part[:], 1.0, positive[:], ALU.mult, ALU.add, accum_out=z[:])
+        inv_z = held.tile([P, 1], F32, name="inv_z")
+        nc.vector.reciprocal(inv_z[:], z[:])
+        share = held.tile([P, G, HALVES], F32, name="share")
+        nc.vector.scalar_tensor_tensor(
+            share[:],
+            quota[:, 0:G].unsqueeze(2).to_broadcast([P, G, HALVES]),
+            inv_z[:],
+            inv_page_sum[:].unsqueeze(2).to_broadcast([P, G, HALVES]),
+            ALU.mult,
+            ALU.mult,
+        )
+        share_turned = psum.tile([P, Q], F32, name="share_turned")
+        nc.tensor.transpose(share_turned[:], share[:].rearrange("q g h -> q (g h)"), identity[:])
+
+        values_block(2)
+
+        w_grouped = held.tile([P, Q, PACK], BF16, name="w_grouped", align_bytes=64)
+        nc.vector.tensor_tensor(
+            w_grouped[:],
+            pa_os[:].rearrange("p t q -> p q t"),
+            share_turned[:].unsqueeze(2).to_broadcast([P, Q, PACK]),
+            ALU.mult,
+        )
+        w_codes = held.tile([P, Q], U32, name="w_codes", align_bytes=64)
+        w_scales = held.tile([P, Q], U8, name="w_scales", align_bytes=64)
+        nc.vector.quantize_mx(
+            out=w_codes[:].bitcast(FP8X4), scales=w_scales[:], in_=w_grouped[:].rearrange("p q t -> p (q t)")
+        )
+
+        def product(name, parts):
+            first, last = parts[0][0], parts[-1][1]
+            bank = psum.tile([P, last - first], F32, name="out_bank_" + name)
+            for lo, hi in parts:
+                nc.tensor.matmul_mx(
+                    out=bank[:, lo - first : hi - first],
+                    lhsT=w_codes[:].bitcast(FP8X4),
+                    lhsT_scale=w_scales[:],
+                    rhs=v_codes[:, lo:hi].bitcast(FP8X4),
+                    rhs_scale=v_scales[:, lo:hi],
+                    start=True,
+                    stop=True,
+                )
+            result = held.tile([P, last - first], F32, name="result_" + name)
+            nc.scalar.copy(result[:], bank[:])
+            nc.sync.dma_start(out[:, first:last], result[:])
+
+        product("early", [(0, 2 * P), (2 * P, 3 * P)])
+        values_block(3)
+        product("last", [(3 * P, 4 * P)])

@@ -30,55 +30,57 @@ def tile_attend_pagequotas_kernel(tc, query, query2, keys_words, keys_scales, re
     with ExitStack() as ctx:
         held = ctx.enter_context(tc.tile_pool(name="held", bufs=1))
         psum = ctx.enter_context(tc.psum_pool(name="psum", bufs=1))
-        turn = ctx.enter_context(tc.psum_pool(name="turn", bufs=2))
+
+        def sbuf(shape, dtype, name, tag=None):
+            return held.tile(shape, dtype, name=name, tag=tag or name, align_bytes=64)
 
         offsets = held.tile([P, I // 16], U16, name="offsets")
         nc.sync.dma_start(offsets[:], offs)
 
-        key_bytes = held.tile([P, T], U8, name="key_bytes")
+        key_bytes = sbuf([P, T], U8, "key_bytes")
         nc.gpsimd.memset(key_bytes[:].bitcast(I32), 0)
-        identity = held.tile([P, P], F32, name="identity")
+        identity = sbuf([P, P], F32, "identity")
         make_identity(nc, identity[:])
-        key_words = held.tile([P, T], U16, name="key_words", tag="slot1")
+        key_words = sbuf([P, T], U16, "key_words", "slot1")
         nc.sync.dma_start(key_words[:].bitcast(I32), keys_words[0].bitcast(I32))
-        for r in range(4):
-            nc.scalar.dma_start(key_bytes[r:P:32, :].bitcast(I32), keys_scales[0, r:16:4, :].bitcast(I32))
 
         q_raw = []
         for n, source in enumerate((query, query2)):
-            raw = held.tile([P, PACK, Q], F32, name="q_raw%d" % n, tag="slot%d" % (n + 2))
+            raw = sbuf([P, PACK, Q], F32, "q_raw%d" % n, "slot%d" % (n + 2))
             nc.sync.dma_start(raw[:], source.rearrange("(p j) q -> p j q", j=PACK))
             q_raw.append(raw)
 
-        factor_cols = held.tile([P, PACK], F32, name="factor_cols")
+        positive = sbuf([P, G + 1], F32, "positive")
+        nc.gpsimd.dma_start(positive[:, G : G + 1], reserve)
+        factor_cols = sbuf([P, PACK], F32, "factor_cols")
         nc.gpsimd.dma_start(factor_cols[:], slot_factors.rearrange("o (p t) -> (o p) t", t=PACK))
-        row_reserve = held.tile([P, 1], F32, name="row_reserve")
-        nc.gpsimd.dma_start(row_reserve[:], reserve)
+        for r in range(4):
+            nc.scalar.dma_start(key_bytes[r:P:32, :].bitcast(I32), keys_scales[0, r:16:4, :].bitcast(I32))
 
         pools = []
 
         def load_values(c):
-            pool_c = held.tile([P, T], F32, name="vals%d" % c, tag="slot%d" % c)
+            pool_c = sbuf([P, T], F32, "vals%d" % c, "slot%d" % c)
             nc.sync.dma_start(pool_c[:], vals[c * P : (c + 1) * P, :])
             pools.append(pool_c)
 
         load_values(0)
 
-        listed_words = held.tile([P, I], U16, name="listed_words", align_bytes=64)
+        listed_words = sbuf([P, I], U16, "listed_words")
         nc.vector.tensor_copy(listed_words[:], key_words[:].indirect(offsets[:]))
-        listed_bytes = held.tile([P, I], U8, name="listed_bytes", align_bytes=64)
+        listed_bytes = sbuf([P, I], U8, "listed_bytes")
         nc.vector.tensor_copy(listed_bytes[:], key_bytes[:].indirect(offsets[:]))
 
         scores = []
         for n in range(2):
-            grouped = held.tile([P, Q, PACK], BF16, name="q_grouped%d" % n, align_bytes=64)
+            grouped = sbuf([P, Q, PACK], BF16, "q_grouped%d" % n)
             nc.scalar.activation(grouped[:], q_raw[n][:].rearrange("p j q -> p q j"), ACT.Copy)
-            codes = held.tile([P, Q], U32, name="q_codes%d" % n, align_bytes=64)
-            scales = held.tile([P, Q], U8, name="q_scales%d" % n, align_bytes=64)
+            codes = sbuf([P, Q], U32, "q_codes%d" % n)
+            scales = sbuf([P, Q], U8, "q_scales%d" % n)
             nc.vector.quantize_mx(
                 out=codes[:].bitcast(FP8X4), scales=scales[:], in_=grouped[:].rearrange("p q j -> p (q j)")
             )
-            bank = psum.tile([P, I], F32, name="scores%d" % n)
+            bank = psum.tile([P, I], F32, name="scores%d" % n, tag="bank%d" % n)
             nc.tensor.matmul_mx(
                 out=bank[:],
                 lhsT=codes[:].bitcast(FP8X4),
@@ -93,70 +95,93 @@ def tile_attend_pagequotas_kernel(tc, query, query2, keys_words, keys_scales, re
         for c in range(1, BLOCKS):
             load_values(c)
 
-        v_codes = held.tile([P, E], U32, name="v_codes", align_bytes=64)
-        v_scales = held.tile([P, E], U8, name="v_scales", align_bytes=64)
+        v_grouped, v_codes, v_scales = [], [], []
 
-        def values_block(c):
-            listed = held.tile([P, I], BF16, name="v_listed%d" % c, align_bytes=64)
+        def gather_values(c, listed_tag, bank_tag, grouped_tag):
+            listed = sbuf([P, I], BF16, "v_listed%d" % c, listed_tag)
             nc.vector.tensor_copy(listed[:], pools[c][:].indirect(offsets[:]))
             pairs = listed[:].bitcast(F32)
-            turned = turn.tile([P, 2, P], F32, name="v_turned")
+            turned = psum.tile([P, 2, P], F32, name="v_turned%d" % c, tag=bank_tag)
             for u in range(2):
                 nc.tensor.transpose(turned[:, u, :], pairs[:, u : I // 2 : 2], identity[:])
-            grouped = held.tile([P, P * PACK], BF16, name="v_grouped%d" % c, align_bytes=64)
+            grouped = sbuf([P, P * PACK], BF16, "v_grouped%d" % c, grouped_tag)
             nc.scalar.copy(
                 grouped[:].bitcast(F32).rearrange("p (e u) -> p e u", u=2), turned[:].rearrange("p u e -> p e u")
             )
-            cols = slice(c * P, (c + 1) * P)
-            nc.vector.quantize_mx(out=v_codes[:, cols].bitcast(FP8X4), scales=v_scales[:, cols], in_=grouped[:])
+            v_grouped.append(grouped)
 
-        page_max = held.tile([P, G], F32, name="page_max")
-        nc.vector.tensor_reduce(page_max[:], a[:].rearrange("q (g j) -> q g j", j=PAGE), AXIS.X, ALU.max)
-        shifted = held.tile([P, PACK, G, HALVES], F32, name="shifted")
-        nc.vector.tensor_tensor(
-            shifted[:],
-            a[:].rearrange("q (g h t) -> q t g h", h=HALVES, t=PACK),
-            page_max[:].unsqueeze(1).unsqueeze(3).to_broadcast([P, PACK, G, HALVES]),
-            ALU.subtract,
-        )
-        b_sum = held.tile([P, G], F32, name="b_sum")
-        nc.vector.tensor_reduce(b_sum[:], b[:].rearrange("q (g j) -> q g j", j=PAGE), AXIS.X, ALU.add)
+        def quantize_values(c, codes_tag):
+            codes = sbuf([P, P], U32, "v_codes%d" % c, codes_tag)
+            scales = sbuf([P, P], U8, "v_scales%d" % c)
+            nc.vector.quantize_mx(out=codes[:].bitcast(FP8X4), scales=scales[:], in_=v_grouped[c][:])
+            v_codes.append(codes)
+            v_scales.append(scales)
 
-        values_block(0)
+        a_dealt = sbuf([P, PACK, P], F32, "a_dealt")
+        nc.scalar.copy(a_dealt[:], a[:].rearrange("q (s t) -> q t s", t=PACK))
 
-        size = held.tile([P, G], F32, name="size")
-        nc.scalar.activation(size[:], b_sum[:], ACT.Abs, scale=3.0 / PAGE)
-        tail = held.tile([P, G], F32, name="tail")
-        nc.scalar.activation(tail[:], size[:], ACT.Exp, scale=-1.0)
-        pa = held.tile([P, PACK, G, HALVES], F32, name="pa")
+        gather_values(0, None, "bank_even", "grouped0")
+
+        page_stats = sbuf([P, 2, G], F32, "page_stats", "slot0")
+        minus_max = page_stats[:, 0, :]
+        b_sum = page_stats[:, 1, :]
+        nc.vector.tensor_reduce(minus_max, a[:].rearrange("q (g j) -> q g j", j=PAGE), AXIS.X, ALU.max, negate=True)
+        minus_max2 = sbuf([P, G, HALVES], F32, "minus_max2", "late_log")
+        nc.scalar.copy(minus_max2[:], minus_max.unsqueeze(2).to_broadcast([P, G, HALVES]))
+        shifted = psum.tile([P, PACK, Q], F32, name="shifted", tag="bank_odd")
+        for t in range(PACK):
+            nc.tensor.matmul(
+                shifted[:, t, :], a_dealt[:, t, :], identity[:], start=(t == 0), stop=False, is_transpose=True
+            )
+        for t in range(PACK):
+            nc.tensor.matmul(
+                shifted[:, t, :],
+                minus_max2[:].rearrange("q g h -> q (g h)"),
+                identity[:],
+                start=False,
+                stop=(t == PACK - 1),
+                is_transpose=True,
+            )
+
+        nc.vector.tensor_reduce(b_sum, b[:].rearrange("q (g j) -> q g j", j=PAGE), AXIS.X, ALU.add)
+        size = sbuf([P, G], F32, "size")
+        nc.scalar.activation(size[:], b_sum, ACT.Abs, scale=3.0 / PAGE)
+        tail = sbuf([P, G + 1], F32, "tail", "after_log")
+        nc.gpsimd.memset(tail[:, G : G + 1], 0.0)
+        nc.scalar.activation(tail[:, 0:G], size[:], ACT.Exp, scale=-1.0)
+
+        pa = sbuf([P, PACK, Q], F32, "pa", "after_factor")
         nc.scalar.activation(pa[:], shifted[:], ACT.Exp)
-        positive = held.tile([P, G + 1], F32, name="positive")
-        nc.scalar.activation(positive[:, 0:G], b_sum[:], ACT.Relu, scale=3.0 / PAGE)
-        nc.scalar.copy(positive[:, G : G + 1], row_reserve[:])
-        log_part = held.tile([P, G + 1], F32, name="log_part")
-        nc.vector.memset(log_part[:, G : G + 1], 0.0)
-        nc.scalar.activation(log_part[:, 0:G], tail[:], ACT.Ln, bias=1.0)
+        log_part = sbuf([P, G + 1], F32, "log_part", "late_log")
+        nc.scalar.activation(log_part[:], tail[:], ACT.Ln, bias=1.0)
+        nc.scalar.activation(positive[:, 0:G], b_sum, ACT.Relu, scale=3.0 / PAGE)
 
-        page_sum = held.tile([P, G], F32, name="page_sum")
-        nc.vector.tensor_reduce(page_sum[:], pa[:].rearrange("q t g h -> q g t h"), AXIS.XY, ALU.add)
-        inv_page_sum = held.tile([P, G], F32, name="inv_page_sum")
+        half_sum = psum.tile([P, P], F32, name="half_sum", tag="small")
+        for t in range(PACK):
+            nc.tensor.matmul(
+                half_sum[:], pa[:, t, :], identity[:], start=(t == 0), stop=(t == PACK - 1), is_transpose=True
+            )
+
+        quantize_values(0, None)
+        gather_values(1, "grouped0", "bank_odd", "after_log")
+
+        pa_os = sbuf([P, PACK, Q], F32, "pa_os")
+        for t in range(PACK):
+            nc.scalar.activation(pa_os[:, t, :], pa[:, t, :], ACT.Copy, scale=factor_cols[:, t : t + 1])
+
+        gather_values(2, None, "bank_even", "after_factor")
+
+        page_sum = sbuf([P, G], F32, "page_sum", "slot2")
+        nc.vector.tensor_reduce(page_sum[:], half_sum[:].rearrange("q (g h) -> q g h", h=HALVES), AXIS.X, ALU.add)
+        inv_page_sum = sbuf([P, G], F32, "inv_page_sum")
         nc.vector.reciprocal(inv_page_sum[:], page_sum[:])
 
-        pa_turned = psum.tile([P, PACK, Q], F32, name="pa_turned")
-        for t in range(PACK):
-            nc.tensor.transpose(pa_turned[:, t, :], pa[:, t, :, :].rearrange("q g h -> q (g h)"), identity[:])
-        pa_os = held.tile([P, PACK, Q], F32, name="pa_os")
-        for t in range(PACK):
-            nc.scalar.activation(pa_os[:, t, :], pa_turned[:, t, :], ACT.Copy, scale=factor_cols[:, t : t + 1])
-
-        values_block(1)
-
-        quota = held.tile([P, G + 1], F32, name="quota")
-        z = held.tile([P, 1], F32, name="z")
+        quota = sbuf([P, G + 1], F32, "quota", "slot2")
+        z = sbuf([P, 1], F32, "z")
         nc.vector.scalar_tensor_tensor(quota[:], log_part[:], 1.0, positive[:], ALU.mult, ALU.add, accum_out=z[:])
-        inv_z = held.tile([P, 1], F32, name="inv_z")
+        inv_z = sbuf([P, 1], F32, "inv_z")
         nc.vector.reciprocal(inv_z[:], z[:])
-        share = held.tile([P, G, HALVES], F32, name="share")
+        share = sbuf([P, G, HALVES], F32, "share", "after_share")
         nc.vector.scalar_tensor_tensor(
             share[:],
             quota[:, 0:G].unsqueeze(2).to_broadcast([P, G, HALVES]),
@@ -165,41 +190,42 @@ def tile_attend_pagequotas_kernel(tc, query, query2, keys_words, keys_scales, re
             ALU.mult,
             ALU.mult,
         )
-        share_turned = psum.tile([P, Q], F32, name="share_turned")
+        share_turned = psum.tile([P, Q], F32, name="share_turned", tag="small")
         nc.tensor.transpose(share_turned[:], share[:].rearrange("q g h -> q (g h)"), identity[:])
 
-        values_block(2)
-
-        w_grouped = held.tile([P, Q, PACK], BF16, name="w_grouped", align_bytes=64)
+        gather_values(3, None, "bank_odd", None)
+        w_grouped = sbuf([P, Q, PACK], BF16, "w_grouped", "slot3")
         nc.vector.tensor_tensor(
             w_grouped[:],
             pa_os[:].rearrange("p t q -> p q t"),
             share_turned[:].unsqueeze(2).to_broadcast([P, Q, PACK]),
             ALU.mult,
         )
-        w_codes = held.tile([P, Q], U32, name="w_codes", align_bytes=64)
-        w_scales = held.tile([P, Q], U8, name="w_scales", align_bytes=64)
+        quantize_values(1, "slot2")
+        quantize_values(2, "after_share")
+        w_codes = sbuf([P, Q], U32, "w_codes")
+        w_scales = sbuf([P, Q], U8, "w_scales")
         nc.vector.quantize_mx(
             out=w_codes[:].bitcast(FP8X4), scales=w_scales[:], in_=w_grouped[:].rearrange("p q t -> p (q t)")
         )
 
-        def product(name, parts):
-            first, last = parts[0][0], parts[-1][1]
-            bank = psum.tile([P, last - first], F32, name="out_bank_" + name)
-            for lo, hi in parts:
+        def product(name, tag, blocks, copy):
+            width = len(blocks) * P
+            bank = psum.tile([P, width], F32, name="out_bank_" + name, tag=tag)
+            for n, c in enumerate(blocks):
                 nc.tensor.matmul_mx(
-                    out=bank[:, lo - first : hi - first],
+                    out=bank[:, n * P : (n + 1) * P],
                     lhsT=w_codes[:].bitcast(FP8X4),
                     lhsT_scale=w_scales[:],
-                    rhs=v_codes[:, lo:hi].bitcast(FP8X4),
-                    rhs_scale=v_scales[:, lo:hi],
+                    rhs=v_codes[c][:].bitcast(FP8X4),
+                    rhs_scale=v_scales[c][:],
                     start=True,
                     stop=True,
                 )
-            result = held.tile([P, last - first], F32, name="result_" + name)
-            nc.scalar.copy(result[:], bank[:])
-            nc.sync.dma_start(out[:, first:last], result[:])
+            result = sbuf([P, width], F32, "result_" + name)
+            copy(result[:], bank[:])
+            nc.sync.dma_start(out[:, blocks[0] * P : blocks[0] * P + width], result[:])
 
-        product("early", [(0, 2 * P), (2 * P, 3 * P)])
-        values_block(3)
-        product("last", [(3 * P, 4 * P)])
+        product("early", "bank0", [0, 1, 2], nc.scalar.copy)
+        quantize_values(3, None)
+        product("last", "bank1", [3], nc.vector.tensor_copy)

from contextlib import ExitStack

import concourse.mybir as mybir
from concourse.masks import make_identity

D, E, T, I, Q, G = 512, 512, 2048, 512, 128, 64
FLOPS = 2 * Q * I * D * 2 + 2 * Q * I * E

F32 = mybir.dt.float32
BF16 = mybir.dt.bfloat16
I32 = mybir.dt.int32
U32 = mybir.dt.uint32
U16 = mybir.dt.uint16
U8 = mybir.dt.uint8
FP8X4 = mybir.dt.float8_e4m3fn_x4
FP4X4 = mybir.dt.float4_e2m1fn_x4
ACT = mybir.ActivationFunctionType
ALU = mybir.AluOpType
AXIS = mybir.AxisListType

P = 128
PACK = 4
PAGE = I // G
HALVES = PAGE // PACK
BLOCKS = E // P


def tile_attend_pagequotas_kernel(tc, query, query2, keys_words, keys_scales, reserve, slot_factors, vals, offs, out):
    nc = tc.nc
    with ExitStack() as ctx:
        held = ctx.enter_context(tc.tile_pool(name="held", bufs=1))
        psum = ctx.enter_context(tc.psum_pool(name="psum", bufs=1))

        def sbuf(shape, dtype, name, tag=None):
            return held.tile(shape, dtype, name=name, tag=tag or name, align_bytes=64)

        offsets = held.tile([P, I // 16], U16, name="offsets")
        nc.sync.dma_start(offsets[:], offs)

        key_bytes = sbuf([P, T], U8, "key_bytes")
        nc.gpsimd.memset(key_bytes[:].bitcast(I32), 0)
        identity = sbuf([P, P], F32, "identity")
        make_identity(nc, identity[:])
        key_words = sbuf([P, T], U16, "key_words", "slot1")
        nc.sync.dma_start(key_words[:].bitcast(I32), keys_words[0].bitcast(I32))

        q_raw = []
        for n, source in enumerate((query, query2)):
            raw = sbuf([P, PACK, Q], F32, "q_raw%d" % n, "slot%d" % (n + 2))
            nc.sync.dma_start(raw[:], source.rearrange("(p j) q -> p j q", j=PACK))
            q_raw.append(raw)

        positive = sbuf([P, G + 1], F32, "positive")
        nc.gpsimd.dma_start(positive[:, G : G + 1], reserve)
        factor_cols = sbuf([P, PACK], F32, "factor_cols")
        nc.gpsimd.dma_start(factor_cols[:], slot_factors.rearrange("o (p t) -> (o p) t", t=PACK))
        for r in range(4):
            nc.scalar.dma_start(key_bytes[r:P:32, :].bitcast(I32), keys_scales[0, r:16:4, :].bitcast(I32))

        pools = []

        def load_values(c):
            pool_c = sbuf([P, T], F32, "vals%d" % c, "slot%d" % c)
            nc.sync.dma_start(pool_c[:], vals[c * P : (c + 1) * P, :])
            pools.append(pool_c)

        load_values(0)

        listed_words = sbuf([P, I], U16, "listed_words")
        nc.vector.tensor_copy(listed_words[:], key_words[:].indirect(offsets[:]))
        listed_bytes = sbuf([P, I], U8, "listed_bytes")
        nc.vector.tensor_copy(listed_bytes[:], key_bytes[:].indirect(offsets[:]))

        scores = []
        for n in range(2):
            grouped = sbuf([P, Q, PACK], BF16, "q_grouped%d" % n)
            nc.scalar.activation(grouped[:], q_raw[n][:].rearrange("p j q -> p q j"), ACT.Copy)
            codes = sbuf([P, Q], U32, "q_codes%d" % n)
            scales = sbuf([P, Q], U8, "q_scales%d" % n)
            nc.vector.quantize_mx(
                out=codes[:].bitcast(FP8X4), scales=scales[:], in_=grouped[:].rearrange("p q j -> p (q j)")
            )
            bank = psum.tile([P, I], F32, name="scores%d" % n, tag="bank%d" % n)
            nc.tensor.matmul_mx(
                out=bank[:],
                lhsT=codes[:].bitcast(FP8X4),
                lhsT_scale=scales[:],
                rhs=listed_words[:].bitcast(FP4X4),
                rhs_scale=listed_bytes[:],
                start=True,
                stop=True,
            )
            scores.append(bank)
        a, b = scores
        for c in range(1, BLOCKS):
            load_values(c)

        v_grouped, v_codes, v_scales = [], [], []

        def gather_values(c, listed_tag, bank_tag, grouped_tag):
            listed = sbuf([P, I], BF16, "v_listed%d" % c, listed_tag)
            nc.vector.tensor_copy(listed[:], pools[c][:].indirect(offsets[:]))
            pairs = listed[:].bitcast(F32)
            turned = psum.tile([P, 2, P], F32, name="v_turned%d" % c, tag=bank_tag)
            for u in range(2):
                nc.tensor.transpose(turned[:, u, :], pairs[:, u : I // 2 : 2], identity[:])
            grouped = sbuf([P, P * PACK], BF16, "v_grouped%d" % c, grouped_tag)
            nc.scalar.copy(
                grouped[:].bitcast(F32).rearrange("p (e u) -> p e u", u=2), turned[:].rearrange("p u e -> p e u")
            )
            v_grouped.append(grouped)

        def quantize_values(c, codes_tag):
            codes = sbuf([P, P], U32, "v_codes%d" % c, codes_tag)
            scales = sbuf([P, P], U8, "v_scales%d" % c)
            nc.vector.quantize_mx(out=codes[:].bitcast(FP8X4), scales=scales[:], in_=v_grouped[c][:])
            v_codes.append(codes)
            v_scales.append(scales)

        a_dealt = sbuf([P, PACK, P], F32, "a_dealt")
        nc.scalar.copy(a_dealt[:], a[:].rearrange("q (s t) -> q t s", t=PACK))

        gather_values(0, None, "bank_even", "grouped0")

        page_stats = sbuf([P, 2, G], F32, "page_stats", "slot0")
        minus_max = page_stats[:, 0, :]
        b_sum = page_stats[:, 1, :]
        nc.vector.tensor_reduce(minus_max, a[:].rearrange("q (g j) -> q g j", j=PAGE), AXIS.X, ALU.max, negate=True)
        minus_max2 = sbuf([P, G, HALVES], F32, "minus_max2", "late_log")
        nc.scalar.copy(minus_max2[:], minus_max.unsqueeze(2).to_broadcast([P, G, HALVES]))
        shifted = psum.tile([P, PACK, Q], F32, name="shifted", tag="bank_odd")
        for t in range(PACK):
            nc.tensor.matmul(
                shifted[:, t, :], a_dealt[:, t, :], identity[:], start=(t == 0), stop=False, is_transpose=True
            )
        for t in range(PACK):
            nc.tensor.matmul(
                shifted[:, t, :],
                minus_max2[:].rearrange("q g h -> q (g h)"),
                identity[:],
                start=False,
                stop=(t == PACK - 1),
                is_transpose=True,
            )

        nc.vector.tensor_reduce(b_sum, b[:].rearrange("q (g j) -> q g j", j=PAGE), AXIS.X, ALU.add)
        size = sbuf([P, G], F32, "size")
        nc.scalar.activation(size[:], b_sum, ACT.Abs, scale=3.0 / PAGE)
        tail = sbuf([P, G + 1], F32, "tail", "after_log")
        nc.gpsimd.memset(tail[:, G : G + 1], 0.0)
        nc.scalar.activation(tail[:, 0:G], size[:], ACT.Exp, scale=-1.0)

        pa = sbuf([P, PACK, Q], F32, "pa", "after_factor")
        nc.scalar.activation(pa[:], shifted[:], ACT.Exp)
        log_part = sbuf([P, G + 1], F32, "log_part", "late_log")
        nc.scalar.activation(log_part[:], tail[:], ACT.Ln, bias=1.0)
        nc.scalar.activation(positive[:, 0:G], b_sum, ACT.Relu, scale=3.0 / PAGE)

        half_sum = psum.tile([P, P], F32, name="half_sum", tag="small")
        for t in range(PACK):
            nc.tensor.matmul(
                half_sum[:], pa[:, t, :], identity[:], start=(t == 0), stop=(t == PACK - 1), is_transpose=True
            )

        quantize_values(0, None)
        gather_values(1, "grouped0", "bank_odd", "after_log")

        pa_os = sbuf([P, PACK, Q], F32, "pa_os")
        for t in range(PACK):
            nc.scalar.activation(pa_os[:, t, :], pa[:, t, :], ACT.Copy, scale=factor_cols[:, t : t + 1])

        gather_values(2, None, "bank_even", "after_factor")

        page_sum = sbuf([P, G], F32, "page_sum", "slot2")
        nc.vector.tensor_reduce(page_sum[:], half_sum[:].rearrange("q (g h) -> q g h", h=HALVES), AXIS.X, ALU.add)
        inv_page_sum = sbuf([P, G], F32, "inv_page_sum")
        nc.vector.reciprocal(inv_page_sum[:], page_sum[:])

        quota = sbuf([P, G + 1], F32, "quota", "slot2")
        z = sbuf([P, 1], F32, "z")
        nc.vector.scalar_tensor_tensor(quota[:], log_part[:], 1.0, positive[:], ALU.mult, ALU.add, accum_out=z[:])
        inv_z = sbuf([P, 1], F32, "inv_z")
        nc.vector.reciprocal(inv_z[:], z[:])
        share = sbuf([P, G, HALVES], F32, "share", "after_share")
        nc.vector.scalar_tensor_tensor(
            share[:],
            quota[:, 0:G].unsqueeze(2).to_broadcast([P, G, HALVES]),
            inv_z[:],
            inv_page_sum[:].unsqueeze(2).to_broadcast([P, G, HALVES]),
            ALU.mult,
            ALU.mult,
        )
        share_turned = psum.tile([P, Q], F32, name="share_turned", tag="small")
        nc.tensor.transpose(share_turned[:], share[:].rearrange("q g h -> q (g h)"), identity[:])

        gather_values(3, None, "bank_odd", None)
        w_grouped = sbuf([P, Q, PACK], BF16, "w_grouped", "slot3")
        nc.vector.tensor_tensor(
            w_grouped[:],
            pa_os[:].rearrange("p t q -> p q t"),
            share_turned[:].unsqueeze(2).to_broadcast([P, Q, PACK]),
            ALU.mult,
        )
        quantize_values(1, "slot2")
        quantize_values(2, "after_share")
        w_codes = sbuf([P, Q], U32, "w_codes")
        w_scales = sbuf([P, Q], U8, "w_scales")
        nc.vector.quantize_mx(
            out=w_codes[:].bitcast(FP8X4), scales=w_scales[:], in_=w_grouped[:].rearrange("p q t -> p (q t)")
        )

        def product(name, tag, blocks, copy):
            width = len(blocks) * P
            bank = psum.tile([P, width], F32, name="out_bank_" + name, tag=tag)
            for n, c in enumerate(blocks):
                nc.tensor.matmul_mx(
                    out=bank[:, n * P : (n + 1) * P],
                    lhsT=w_codes[:].bitcast(FP8X4),
                    lhsT_scale=w_scales[:],
                    rhs=v_codes[c][:].bitcast(FP8X4),
                    rhs_scale=v_scales[c][:],
                    start=True,
                    stop=True,
                )
            result = sbuf([P, width], F32, "result_" + name)
            copy(result[:], bank[:])
            nc.sync.dma_start(out[:, blocks[0] * P : blocks[0] * P + width], result[:])

        product("early", "bank0", [0, 1, 2], nc.scalar.copy)
        quantize_values(3, None)
        product("last", "bank1", [3], nc.vector.tensor_copy)
